import numpy as np
import ml_dtypes


def mxq(x, axis, fmt="e4m3"):
    dtype, down = {"e4m3": (ml_dtypes.float8_e4m3fn, 7), "e5m2": (ml_dtypes.float8_e5m2, 14)}[fmt]
    v = np.moveaxis(np.asarray(x, np.float32).astype(ml_dtypes.bfloat16).astype(np.float64), axis, -1)
    blocks = v.reshape(v.shape[:-1] + (-1, 32))
    amax = np.abs(blocks).max(-1, keepdims=True)
    byte = np.maximum(np.where(amax > 0, np.frexp(amax)[1] - 1 + 127, 0) - down, 1)
    scale = np.exp2(byte - 127.0)
    codes = (blocks / scale).astype(np.float32).astype(dtype).astype(np.float64)
    return np.moveaxis((codes * scale).reshape(v.shape), -1, axis)


WIDE = False


def mx_kscale(k):
    if not WIDE:
        return np.ones(k)
    levels = np.array([10, -10, 5, -5, 0])
    if k % 512:
        return np.exp2(np.random.permutation(np.resize(levels, k // 32))).repeat(32)
    a = np.empty((k // 512, 16))
    for p in range(k // 512):
        a[p, :8] = np.random.permutation(np.resize(levels, 8))
        for g in range(8):
            far = levels[np.abs(levels - a[p, g]) >= 10]
            a[p, g + 8] = far[np.random.randint(len(far))]
    return np.exp2(a.ravel()).repeat(32)


def f64(x):
    return np.asarray(x).astype(np.float64)


E2M1 = np.array([0.0, 0.5, 1.0, 1.5, 2.0, 3.0, 4.0, 6.0, -0.0, -0.5, -1.0, -1.5, -2.0, -3.0, -4.0, -6.0])


def pack_weight(w, fmt):
    k, n = w.shape
    w = f64(np.asarray(w, np.float32).astype(ml_dtypes.bfloat16)).reshape(k // 32, 32, n)
    amax = np.abs(w).max(1)
    if fmt == "e4m3":
        byte = np.frexp(amax)[1] - 1 + 127 - 7
    else:
        mant, ex = np.frexp(amax / 6.0)
        byte = np.where(mant > 0.5, ex, ex - 1) + 127
    byte = np.clip(np.where(amax > 0, byte, 1), 1, 254)
    scaled = (w * np.exp2(127.0 - byte)[:, None, :]).reshape(k, n).astype(np.float32)
    by_word = np.ascontiguousarray(scaled.reshape(k // 512, 128, 4, n).transpose(0, 1, 3, 2))
    if fmt == "e4m3":
        words = by_word.astype(ml_dtypes.float8_e4m3fn).view(np.uint8)
    else:
        c = by_word.astype(ml_dtypes.float4_e2m1fn).view(np.uint8) & 0xF
        words = (c[..., 0::2] | (c[..., 1::2] << 4)).reshape(k // 512, 128, 2 * n)
    return np.ascontiguousarray(words), np.ascontiguousarray(byte.astype(np.uint8).reshape(k // 512, 16, n))


def unpack_weight(words, scales, fmt):
    g, _, n = scales.shape
    words = np.ascontiguousarray(words).reshape(g, 128, n, -1)
    if fmt == "e4m3":
        vals = words.view(ml_dtypes.float8_e4m3fn).astype(np.float64)
    else:
        nib = np.empty((g, 128, n, 4), np.uint8)
        nib[..., 0::2] = words & 0xF
        nib[..., 1::2] = words >> 4
        vals = E2M1[nib]
    vals = vals * np.repeat(np.exp2(scales.astype(np.float64) - 127.0), 8, axis=1)[..., None]
    return vals.transpose(0, 1, 3, 2).reshape(g * 512, n)


def silu(v):
    return v / (1.0 + np.exp(-np.maximum(v, -700.0)))


K, M, T = 512, 1024, 512


def setup_inputs():
    n = np.random.standard_normal
    s = mx_kscale(K)[:, None]
    p_w4 = pack_weight(n((K, M)) / np.sqrt(K) / s, "e2m1")
    p_w8 = pack_weight(n((K, M)) / np.sqrt(K) / s, "e4m3")
    return {
        "x": (n((K, T)) * s).astype(np.float32),
        "w4_words": p_w4[0],
        "w4_scales": p_w4[1],
        "w8_words": p_w8[0],
        "w8_scales": p_w8[1],
    }


def reference(x, w4_words, w4_scales, w8_words, w8_scales):
    x_ = mxq(f64(x), 0, "e4m3")
    w4_ = unpack_weight(w4_words, w4_scales, "e2m1")
    w8_ = unpack_weight(w8_words, w8_scales, "e4m3")
    y = x_.T @ w4_
    u = x_.T @ w8_
    y = silu(y) * u
    return y

@@ -1,0 +1,150 @@
+from contextlib import ExitStack
+
+import concourse.mybir as mybir
+
+K, N, T = 512, 1024, 512
+
+FLOPS = 2 * (2 * K * N * T)
+
+F32 = mybir.dt.float32
+BF16 = mybir.dt.bfloat16
+I32 = mybir.dt.int32
+U32 = mybir.dt.uint32
+U8 = mybir.dt.uint8
+E4M3X4 = mybir.dt.float8_e4m3fn_x4
+E2M1X4 = mybir.dt.float4_e2m1fn_x4
+ALU = mybir.AluOpType
+ACT = mybir.ActivationFunctionType
+
+P = 128
+M = 128
+HALF = 2 * M
+
+PIECES = [
+    (0, 0, 256),
+    (0, 256, 256),
+    (1, 0, 512),
+    (0, 512, 512),
+    (1, 512, 512),
+    (2, 0, 512),
+    (2, 512, 512),
+    (3, 0, 512),
+    (3, 512, 256),
+    (3, 768, 256),
+]
+
+
+def tile_mix_glu48_tm_none_kernel(tc, x, w4_words, w4_scales, w8_words, w8_scales, out):
+    nc = tc.nc
+    with ExitStack() as ctx:
+        keep = ctx.enter_context(tc.tile_pool(name="keep", bufs=1))
+        psum_g = ctx.enter_context(tc.psum_pool(name="psum_g", bufs=4))
+        psum_u = ctx.enter_context(tc.psum_pool(name="psum_u", bufs=4))
+        ctx.enter_context(tc.manual_schedule())
+
+        def sbuf(shape, dtype, name):
+            return keep.tile(shape, dtype, name=name, tag=name, align_bytes=64)
+
+        plane4 = sbuf([P, N], U8, "plane4")
+        plane8 = sbuf([P, N], U8, "plane8")
+        w4 = sbuf([P, 2 * N], U8, "w4")
+        w8 = sbuf([P, N], U32, "w8")
+        raw = [sbuf([P, 4, HALF], F32, "raw%d" % h) for h in range(2)]
+        grouped = [sbuf([P, M, 4], BF16, "grouped%d" % m) for m in range(4)]
+        codes = [sbuf([P, M], U32, "codes%d" % m) for m in range(4)]
+        scales = [sbuf([P, M], U8, "scales%d" % m) for m in range(4)]
+        warm = sbuf([P, 1], F32, "warm")
+        warm_out = sbuf([P, 1], F32, "warm_out")
+
+        x_rows = x.rearrange("(p j) t -> p j t", j=4)
+        nc.sync.dma_start(out=raw[0][:], in_=x_rows[:, :, 0:HALF])
+        nc.vector.memset(plane4[:].bitcast(I32), 0)
+        nc.gpsimd.memset(plane8[:].bitcast(I32), 0)
+        nc.vector.memset(warm[:], 0.0)
+        for q in range(4):
+            rows = slice(4 * q, 4 * q + 4)
+            live = slice(32 * q, 32 * q + 4)
+            nc.scalar.dma_start(out=plane4[live, :].bitcast(I32), in_=w4_scales[0, rows, :].bitcast(I32))
+            nc.gpsimd.dma_start(out=plane8[live, :].bitcast(I32), in_=w8_scales[0, rows, :].bitcast(I32))
+        nc.sync.dma_start(out=w4[:].bitcast(I32), in_=w4_words[0].bitcast(I32))
+        nc.sync.dma_start(out=w8[:].bitcast(I32), in_=w8_words[0].rearrange("p n i -> p (n i)").bitcast(I32))
+        nc.sync.dma_start(out=raw[1][:], in_=x_rows[:, :, HALF:T])
+        nc.scalar.activation(out=warm_out[:], in_=warm[:], func=ACT.Silu)
+
+        def raw_of(m):
+            c0 = (m % 2) * M
+            return raw[m // 2][:, :, c0 : c0 + M].rearrange("p j t -> p t j")
+
+        def quantize(m):
+            nc.vector.quantize_mx(
+                out=codes[m][:].bitcast(E4M3X4),
+                scales=scales[m][:],
+                in_=grouped[m][:].rearrange("p t j -> p (t j)"),
+            )
+
+        g_sum = {}
+        u_sum = {}
+        gate = {}
+        result = {}
+
+        def gate_pass(i):
+            m, c0, n = PIECES[i]
+            g_sum[i] = psum_g.tile([M, 512], F32, name="g%d" % i, tag="g")
+            nc.tensor.matmul_mx(
+                out=g_sum[i][:, 0:n],
+                lhsT=codes[m][:].bitcast(E4M3X4),
+                lhsT_scale=scales[m][:],
+                rhs=w4[:, 2 * c0 : 2 * (c0 + n)].bitcast(E2M1X4),
+                rhs_scale=plane4[:, c0 : c0 + n],
+                start=True,
+                stop=True,
+            )
+
+        def up_pass(i):
+            m, c0, n = PIECES[i]
+            u_sum[i] = psum_u.tile([M, 512], F32, name="u%d" % i, tag="u")
+            nc.tensor.matmul_mx(
+                out=u_sum[i][:, 0:n],
+                lhsT=codes[m][:].bitcast(E4M3X4),
+                lhsT_scale=scales[m][:],
+                rhs=w8[:, c0 : c0 + n].bitcast(E4M3X4),
+                rhs_scale=plane8[:, c0 : c0 + n],
+                start=True,
+                stop=True,
+            )
+
+        def silu(i):
+            n = PIECES[i][2]
+            gate[i] = sbuf([M, n], F32, "gate%d" % i)
+            nc.scalar.activation(out=gate[i][:], in_=g_sum[i][:, 0:n], func=ACT.Silu)
+
+        def multiply_and_store(i):
+            m, c0, n = PIECES[i]
+            result[i] = sbuf([M, n], F32, "result%d" % i)
+            nc.vector.tensor_tensor(out=result[i][:], in0=u_sum[i][:, 0:n], in1=gate[i][:], op=ALU.mult)
+            nc.sync.dma_start(out=out[m * M : (m + 1) * M, c0 : c0 + n], in_=result[i][:])
+
+        nc.vector.tensor_copy(out=grouped[0][:], in_=raw_of(0))
+        nc.scalar.copy(out=grouped[1][:], in_=raw_of(1))
+        quantize(0)
+        gate_pass(0)
+        gate_pass(1)
+        up_pass(0)
+        quantize(1)
+        nc.gpsimd.tensor_scalar(
+            out=grouped[3][:], in0=raw_of(3), scalar1=1.0, scalar2=0.0, op0=ALU.mult, op1=ALU.add
+        )
+
+        for i in range(len(PIECES)):
+            silu(i)
+            multiply_and_store(i)
+            if i == 2:
+                nc.vector.tensor_copy(out=grouped[2][:], in_=raw_of(2))
+            if i == 3:
+                quantize(2)
+            if i == 4:
+                quantize(3)
+            if i + 1 < len(PIECES):
+                up_pass(i + 1)
+            if i + 2 < len(PIECES):
+                gate_pass(i + 2)

@@ -1,6 +1,7 @@
 from contextlib import ExitStack
 
 import concourse.mybir as mybir
+from concourse.masks import make_identity
 
 K, N, T = 512, 1024, 512
 
@@ -19,12 +20,13 @@ ACT = mybir.ActivationFunctionType
 P = 128
 M = 128
 HALF = 2 * M
+WARM_TRANSPOSES = 8
 
 PIECES = [
     (0, 0, 256),
     (0, 256, 256),
-    (1, 0, 512),
     (0, 512, 512),
+    (1, 0, 512),
     (1, 512, 512),
     (2, 0, 512),
     (2, 512, 512),
@@ -38,7 +40,8 @@ def tile_mix_glu48_tm_none_kernel(tc, x, w4_words, w4_scales, w8_words, w8_scale
     nc = tc.nc
     with ExitStack() as ctx:
         keep = ctx.enter_context(tc.tile_pool(name="keep", bufs=1))
-        psum_g = ctx.enter_context(tc.psum_pool(name="psum_g", bufs=4))
+        psum_w = ctx.enter_context(tc.psum_pool(name="psum_w", bufs=1))
+        psum_g = ctx.enter_context(tc.psum_pool(name="psum_g", bufs=3))
         psum_u = ctx.enter_context(tc.psum_pool(name="psum_u", bufs=4))
         ctx.enter_context(tc.manual_schedule())
 
@@ -49,7 +52,7 @@ def tile_mix_glu48_tm_none_kernel(tc, x, w4_words, w4_scales, w8_words, w8_scale
         plane8 = sbuf([P, N], U8, "plane8")
         w4 = sbuf([P, 2 * N], U8, "w4")
         w8 = sbuf([P, N], U32, "w8")
-        raw = [sbuf([P, 4, HALF], F32, "raw%d" % h) for h in range(2)]
+        raw = [sbuf([P, 4, n], F32, "raw%d" % h) for h, n in enumerate((M, M, HALF))]
         grouped = [sbuf([P, M, 4], BF16, "grouped%d" % m) for m in range(4)]
         codes = [sbuf([P, M], U32, "codes%d" % m) for m in range(4)]
         scales = [sbuf([P, M], U8, "scales%d" % m) for m in range(4)]
@@ -57,23 +60,32 @@ def tile_mix_glu48_tm_none_kernel(tc, x, w4_words, w4_scales, w8_words, w8_scale
         warm_out = sbuf([P, 1], F32, "warm_out")
 
         x_rows = x.rearrange("(p j) t -> p j t", j=4)
-        nc.sync.dma_start(out=raw[0][:], in_=x_rows[:, :, 0:HALF])
-        nc.vector.memset(plane4[:].bitcast(I32), 0)
+        nc.gpsimd.memset(plane4[:].bitcast(I32), 0)
         nc.gpsimd.memset(plane8[:].bitcast(I32), 0)
         nc.vector.memset(warm[:], 0.0)
-        for q in range(4):
-            rows = slice(4 * q, 4 * q + 4)
-            live = slice(32 * q, 32 * q + 4)
-            nc.scalar.dma_start(out=plane4[live, :].bitcast(I32), in_=w4_scales[0, rows, :].bitcast(I32))
-            nc.gpsimd.dma_start(out=plane8[live, :].bitcast(I32), in_=w8_scales[0, rows, :].bitcast(I32))
+        nc.sync.dma_start(out=raw[0][:], in_=x_rows[:, :, 0:128])
+        nc.sync.dma_start(out=plane4[0:4, :].bitcast(I32), in_=w4_scales[0, 0:4, :].bitcast(I32))
+        nc.sync.dma_start(out=plane4[32:36, :].bitcast(I32), in_=w4_scales[0, 4:8, :].bitcast(I32))
+        nc.scalar.dma_start(out=plane4[64:68, :].bitcast(I32), in_=w4_scales[0, 8:12, :].bitcast(I32))
+        nc.scalar.dma_start(out=plane4[96:100, :].bitcast(I32), in_=w4_scales[0, 12:16, :].bitcast(I32))
         nc.sync.dma_start(out=w4[:].bitcast(I32), in_=w4_words[0].bitcast(I32))
         nc.sync.dma_start(out=w8[:].bitcast(I32), in_=w8_words[0].rearrange("p n i -> p (n i)").bitcast(I32))
-        nc.sync.dma_start(out=raw[1][:], in_=x_rows[:, :, HALF:T])
+        nc.sync.dma_start(out=raw[1][:], in_=x_rows[:, :, 128:256])
+        nc.sync.dma_start(out=plane8[0:4, :].bitcast(I32), in_=w8_scales[0, 0:4, :].bitcast(I32))
+        nc.sync.dma_start(out=plane8[32:36, :].bitcast(I32), in_=w8_scales[0, 4:8, :].bitcast(I32))
+        nc.sync.dma_start(out=plane8[64:68, :].bitcast(I32), in_=w8_scales[0, 8:12, :].bitcast(I32))
+        nc.sync.dma_start(out=plane8[96:100, :].bitcast(I32), in_=w8_scales[0, 12:16, :].bitcast(I32))
+        nc.sync.dma_start(out=raw[2][:], in_=x_rows[:, :, 256:512])
+        ident = sbuf([P, P], BF16, "ident")
+        make_identity(nc, ident[:])
+        spin = psum_w.tile([P, WARM_TRANSPOSES * P], BF16, name="spin", tag="spin")
+        for i in range(WARM_TRANSPOSES):
+            nc.tensor.transpose(spin[:, i * P : (i + 1) * P], ident[:], ident[:])
         nc.scalar.activation(out=warm_out[:], in_=warm[:], func=ACT.Silu)
 
         def raw_of(m):
-            c0 = (m % 2) * M
-            return raw[m // 2][:, :, c0 : c0 + M].rearrange("p j t -> p t j")
+            tile, c0 = ((raw[0], 0), (raw[1], 0), (raw[2], 0), (raw[2], M))[m]
+            return tile[:, :, c0 : c0 + M].rearrange("p j t -> p t j")
 
         def quantize(m):
             nc.vector.quantize_mx(
@@ -125,26 +137,52 @@ def tile_mix_glu48_tm_none_kernel(tc, x, w4_words, w4_scales, w8_words, w8_scale
             nc.sync.dma_start(out=out[m * M : (m + 1) * M, c0 : c0 + n], in_=result[i][:])
 
         nc.vector.tensor_copy(out=grouped[0][:], in_=raw_of(0))
-        nc.scalar.copy(out=grouped[1][:], in_=raw_of(1))
         quantize(0)
+        nc.vector.tensor_copy(out=grouped[1][:], in_=raw_of(1))
+        quantize(1)
         gate_pass(0)
         gate_pass(1)
+        gate_pass(2)
         up_pass(0)
-        quantize(1)
+        silu(0)
+        multiply_and_store(0)
+        up_pass(1)
+        silu(1)
+        multiply_and_store(1)
+        up_pass(2)
+        gate_pass(3)
+        silu(2)
         nc.gpsimd.tensor_scalar(
             out=grouped[3][:], in0=raw_of(3), scalar1=1.0, scalar2=0.0, op0=ALU.mult, op1=ALU.add
         )
-
-        for i in range(len(PIECES)):
-            silu(i)
-            multiply_and_store(i)
-            if i == 2:
-                nc.vector.tensor_copy(out=grouped[2][:], in_=raw_of(2))
-            if i == 3:
-                quantize(2)
-            if i == 4:
-                quantize(3)
-            if i + 1 < len(PIECES):
-                up_pass(i + 1)
-            if i + 2 < len(PIECES):
-                gate_pass(i + 2)
+        nc.scalar.copy(out=grouped[2][:], in_=raw_of(2))
+        multiply_and_store(2)
+        up_pass(3)
+        gate_pass(4)
+        silu(3)
+        quantize(2)
+        quantize(3)
+        multiply_and_store(3)
+        up_pass(4)
+        gate_pass(5)
+        silu(4)
+        multiply_and_store(4)
+        up_pass(5)
+        gate_pass(6)
+        silu(5)
+        multiply_and_store(5)
+        up_pass(6)
+        gate_pass(7)
+        silu(6)
+        multiply_and_store(6)
+        up_pass(7)
+        gate_pass(8)
+        silu(7)
+        multiply_and_store(7)
+        up_pass(8)
+        gate_pass(9)
+        silu(8)
+        multiply_and_store(8)
+        up_pass(9)
+        silu(9)
+        multiply_and_store(9)

from contextlib import ExitStack

import concourse.mybir as mybir
from concourse.masks import make_identity

K, N, T = 512, 1024, 512

FLOPS = 2 * (2 * K * N * T)

F32 = mybir.dt.float32
BF16 = mybir.dt.bfloat16
I32 = mybir.dt.int32
U32 = mybir.dt.uint32
U8 = mybir.dt.uint8
E4M3X4 = mybir.dt.float8_e4m3fn_x4
E2M1X4 = mybir.dt.float4_e2m1fn_x4
ALU = mybir.AluOpType
ACT = mybir.ActivationFunctionType

P = 128
M = 128
HALF = 2 * M
WARM_TRANSPOSES = 8

PIECES = [
    (0, 0, 256),
    (0, 256, 256),
    (0, 512, 512),
    (1, 0, 512),
    (1, 512, 512),
    (2, 0, 512),
    (2, 512, 512),
    (3, 0, 512),
    (3, 512, 256),
    (3, 768, 256),
]


def tile_mix_glu48_tm_none_kernel(tc, x, w4_words, w4_scales, w8_words, w8_scales, out):
    nc = tc.nc
    with ExitStack() as ctx:
        keep = ctx.enter_context(tc.tile_pool(name="keep", bufs=1))
        psum_w = ctx.enter_context(tc.psum_pool(name="psum_w", bufs=1))
        psum_g = ctx.enter_context(tc.psum_pool(name="psum_g", bufs=3))
        psum_u = ctx.enter_context(tc.psum_pool(name="psum_u", bufs=4))
        ctx.enter_context(tc.manual_schedule())

        def sbuf(shape, dtype, name):
            return keep.tile(shape, dtype, name=name, tag=name, align_bytes=64)

        plane4 = sbuf([P, N], U8, "plane4")
        plane8 = sbuf([P, N], U8, "plane8")
        w4 = sbuf([P, 2 * N], U8, "w4")
        w8 = sbuf([P, N], U32, "w8")
        raw = [sbuf([P, 4, n], F32, "raw%d" % h) for h, n in enumerate((M, M, HALF))]
        grouped = [sbuf([P, M, 4], BF16, "grouped%d" % m) for m in range(4)]
        codes = [sbuf([P, M], U32, "codes%d" % m) for m in range(4)]
        scales = [sbuf([P, M], U8, "scales%d" % m) for m in range(4)]
        warm = sbuf([P, 1], F32, "warm")
        warm_out = sbuf([P, 1], F32, "warm_out")

        x_rows = x.rearrange("(p j) t -> p j t", j=4)
        nc.gpsimd.memset(plane4[:].bitcast(I32), 0)
        nc.gpsimd.memset(plane8[:].bitcast(I32), 0)
        nc.vector.memset(warm[:], 0.0)
        nc.sync.dma_start(out=raw[0][:], in_=x_rows[:, :, 0:128])
        nc.sync.dma_start(out=plane4[0:4, :].bitcast(I32), in_=w4_scales[0, 0:4, :].bitcast(I32))
        nc.sync.dma_start(out=plane4[32:36, :].bitcast(I32), in_=w4_scales[0, 4:8, :].bitcast(I32))
        nc.scalar.dma_start(out=plane4[64:68, :].bitcast(I32), in_=w4_scales[0, 8:12, :].bitcast(I32))
        nc.scalar.dma_start(out=plane4[96:100, :].bitcast(I32), in_=w4_scales[0, 12:16, :].bitcast(I32))
        nc.sync.dma_start(out=w4[:].bitcast(I32), in_=w4_words[0].bitcast(I32))
        nc.sync.dma_start(out=w8[:].bitcast(I32), in_=w8_words[0].rearrange("p n i -> p (n i)").bitcast(I32))
        nc.sync.dma_start(out=raw[1][:], in_=x_rows[:, :, 128:256])
        nc.sync.dma_start(out=plane8[0:4, :].bitcast(I32), in_=w8_scales[0, 0:4, :].bitcast(I32))
        nc.sync.dma_start(out=plane8[32:36, :].bitcast(I32), in_=w8_scales[0, 4:8, :].bitcast(I32))
        nc.sync.dma_start(out=plane8[64:68, :].bitcast(I32), in_=w8_scales[0, 8:12, :].bitcast(I32))
        nc.sync.dma_start(out=plane8[96:100, :].bitcast(I32), in_=w8_scales[0, 12:16, :].bitcast(I32))
        nc.sync.dma_start(out=raw[2][:], in_=x_rows[:, :, 256:512])
        ident = sbuf([P, P], BF16, "ident")
        make_identity(nc, ident[:])
        spin = psum_w.tile([P, WARM_TRANSPOSES * P], BF16, name="spin", tag="spin")
        for i in range(WARM_TRANSPOSES):
            nc.tensor.transpose(spin[:, i * P : (i + 1) * P], ident[:], ident[:])
        nc.scalar.activation(out=warm_out[:], in_=warm[:], func=ACT.Silu)

        def raw_of(m):
            tile, c0 = ((raw[0], 0), (raw[1], 0), (raw[2], 0), (raw[2], M))[m]
            return tile[:, :, c0 : c0 + M].rearrange("p j t -> p t j")

        def quantize(m):
            nc.vector.quantize_mx(
                out=codes[m][:].bitcast(E4M3X4),
                scales=scales[m][:],
                in_=grouped[m][:].rearrange("p t j -> p (t j)"),
            )

        g_sum = {}
        u_sum = {}
        gate = {}
        result = {}

        def gate_pass(i):
            m, c0, n = PIECES[i]
            g_sum[i] = psum_g.tile([M, 512], F32, name="g%d" % i, tag="g")
            nc.tensor.matmul_mx(
                out=g_sum[i][:, 0:n],
                lhsT=codes[m][:].bitcast(E4M3X4),
                lhsT_scale=scales[m][:],
                rhs=w4[:, 2 * c0 : 2 * (c0 + n)].bitcast(E2M1X4),
                rhs_scale=plane4[:, c0 : c0 + n],
                start=True,
                stop=True,
            )

        def up_pass(i):
            m, c0, n = PIECES[i]
            u_sum[i] = psum_u.tile([M, 512], F32, name="u%d" % i, tag="u")
            nc.tensor.matmul_mx(
                out=u_sum[i][:, 0:n],
                lhsT=codes[m][:].bitcast(E4M3X4),
                lhsT_scale=scales[m][:],
                rhs=w8[:, c0 : c0 + n].bitcast(E4M3X4),
                rhs_scale=plane8[:, c0 : c0 + n],
                start=True,
                stop=True,
            )

        def silu(i):
            n = PIECES[i][2]
            gate[i] = sbuf([M, n], F32, "gate%d" % i)
            nc.scalar.activation(out=gate[i][:], in_=g_sum[i][:, 0:n], func=ACT.Silu)

        def multiply_and_store(i):
            m, c0, n = PIECES[i]
            result[i] = sbuf([M, n], F32, "result%d" % i)
            nc.vector.tensor_tensor(out=result[i][:], in0=u_sum[i][:, 0:n], in1=gate[i][:], op=ALU.mult)
            nc.sync.dma_start(out=out[m * M : (m + 1) * M, c0 : c0 + n], in_=result[i][:])

        nc.vector.tensor_copy(out=grouped[0][:], in_=raw_of(0))
        quantize(0)
        nc.vector.tensor_copy(out=grouped[1][:], in_=raw_of(1))
        quantize(1)
        gate_pass(0)
        gate_pass(1)
        gate_pass(2)
        up_pass(0)
        silu(0)
        multiply_and_store(0)
        up_pass(1)
        silu(1)
        multiply_and_store(1)
        up_pass(2)
        gate_pass(3)
        silu(2)
        nc.gpsimd.tensor_scalar(
            out=grouped[3][:], in0=raw_of(3), scalar1=1.0, scalar2=0.0, op0=ALU.mult, op1=ALU.add
        )
        nc.scalar.copy(out=grouped[2][:], in_=raw_of(2))
        multiply_and_store(2)
        up_pass(3)
        gate_pass(4)
        silu(3)
        quantize(2)
        quantize(3)
        multiply_and_store(3)
        up_pass(4)
        gate_pass(5)
        silu(4)
        multiply_and_store(4)
        up_pass(5)
        gate_pass(6)
        silu(5)
        multiply_and_store(5)
        up_pass(6)
        gate_pass(7)
        silu(6)
        multiply_and_store(6)
        up_pass(7)
        gate_pass(8)
        silu(7)
        multiply_and_store(7)
        up_pass(8)
        gate_pass(9)
        silu(8)
        multiply_and_store(8)
        up_pass(9)
        silu(9)
        multiply_and_store(9)
